import numpy as np
CORES = [1,2,5,6,9,10,13,14,17,18,21,22,25,26,29,30]
N = 16
COUNTS = [[0,0,4,0,0,8,8,8,4,0,8,0,0,8,0,0],[32,0,4,0,0,8,8,0,8,4,0,8,0,0,4,4],[32,8,0,4,8,0,0,0,8,0,0,0,4,4,4,0],[32,4,4,0,0,0,0,0,4,4,4,8,8,0,8,4],[32,4,0,4,0,0,0,8,8,0,4,4,4,8,0,0],[32,8,4,0,0,0,8,8,4,0,4,0,4,0,8,4],[32,0,8,0,4,0,0,4,8,8,4,8,0,8,0,4],[32,4,4,0,4,8,4,0,4,8,4,0,8,4,0,0],[32,0,8,8,4,0,0,8,0,4,8,8,4,8,4,4],[32,8,0,8,8,4,8,4,8,0,4,0,0,4,0,0],[32,4,0,8,8,0,8,4,0,4,0,8,8,4,8,4],[32,4,0,4,0,0,0,8,4,4,4,0,0,0,4,0],[32,4,8,8,0,4,0,0,8,0,0,8,0,4,8,4],[32,0,0,4,8,0,8,0,8,4,4,4,0,0,0,8],[32,8,8,4,4,8,0,0,4,0,4,8,8,0,0,0],[32,8,4,8,0,8,8,4,4,8,0,4,0,4,4,0]]
XW, YW = 100, 480
def setup_inputs(rng):
    return {"x": rng.standard_normal((N, 128, XW), dtype=np.float32)}
def reference(x):
    y = np.full((N, 128, YW), np.nan, x.dtype)
    fill = [0] * N
    for s in range(N):
        o = 0
        for d in range(N):
            c = COUNTS[s][d]
            y[d][:, fill[d]:fill[d] + c] = x[s][:, o:o + c]
            o += c; fill[d] += c
    return {"y": y}

SCRATCH = {"buf": ("sbuf", [128, 96], "float32")}
SEMAPHORES = ["a", "b", "c"]
HZ = 32
W = 96
EXC = {(2, 12): 1, (6, 2): 5}


def _bits(m):
    return [i for i in range(32) if (m >> i) & 1]


def _p2(n):
    k = 1
    while k * 2 <= n:
        k *= 2
    return k


def build(tables, cores, topo):
    CN = tables["COUNTS"]
    N = len(cores)
    R = range(N)
    chip = [topo.chip(c) for c in cores]
    same = lambda a, b: chip[a] == chip[b] or topo.same_plane(chip[a], chip[b])
    isG = [any(topo.may_write(cores[r], cores[o]) for o in R if not same(r, o)) for r in R]
    partner = {}
    for r in R:
        if not isG[r]:
            partner[r] = [g for g in R if isG[g] and chip[g] == chip[r] and topo.die(cores[g]) == topo.die(cores[r])][0]
    xo = [[sum(CN[s][:d]) for d in R] for s in R]
    yo = [[sum(CN[t][d] for t in range(s)) for s in R] for d in R]
    ops = []
    cnt = [{"a": 0, "b": 0, "c": 0} for _ in R]
    rr = [0] * N
    late = [0]

    def q2(r):
        if r and late[0]:
            return "scalar"
        rr[r] ^= 1
        return "sync" if rr[r] else "scalar"

    def ld(r, c0, x0, w, sem, q=None):
        ops.append((r, "ld", q or q2(r), c0, c0 + w, x0, sem))
        cnt[r][sem] += 16

    def st(r, y0, c0, w, sem, q=None):
        ops.append((r, "st", q or q2(r), y0, c0, c0 + w, sem))
        cnt[r][sem] += 16

    def wt(r, sem, q="g"):
        if cnt[r][sem]:
            ops.append((r, "wt", q, sem, cnt[r][sem]))

    def wtq(r, sem):
        if r == 0:
            wt(r, sem, "sync")
        wt(r, sem, "scalar")

    def alloc(r, dsts, one=False, high=False):
        full = max(topo.mask(cores[r], cores[d]) for d in dsts)
        low = min(topo.mask(cores[r], cores[o]) for o in R if o != r)
        off = [i for i, d in enumerate(dsts) if topo.mask(cores[r], cores[d]) == low and low != full]
        if full == low:
            off = list(range(len(dsts)))
        on = [i for i in range(len(dsts)) if i not in off]
        L = _bits(low)
        H = [b for b in _bits(full) if b not in L]
        out = [0] * len(dsts)
        if off:
            k = 1 if one else _p2(len(L) // len(off))
            for j, i in enumerate(off):
                out[i] = sum(1 << b for b in L[j * k:(j + 1) * k])
        if on:
            pool = H if (off or high) else L + H
            k = 1 if one else _p2(len(pool) // len(on))
            for j, i in enumerate(on):
                out[i] = sum(1 << b for b in pool[j * k:(j + 1) * k])
        return out

    def snd(r, trs, rsem, lsem, high=False):
        ms = alloc(r, [t[0] for t in trs], high=high)
        ops.append((r, "snd", "g", [(t[0], t[1], t[2], t[3], m) for t, m in zip(trs, ms)], rsem, lsem))
        for t, m in zip(trs, ms):
            k = len(_bits(m))
            cnt[t[0]][rsem] += k
            cnt[r][lsem] += k

    def sg(r, dsts, rsem, lsem):
        ms = alloc(r, dsts, one=True)
        ops.append((r, "sg", "g", list(zip(dsts, ms)), rsem, lsem))
        for d in dsts:
            cnt[d][rsem] += 1
            cnt[r][lsem] += 1

    def small(s, d):
        return d != 0 and CN[s][d] > 0

    cls = {}
    for s in R:
        for d in R:
            if small(s, d):
                cls[(s, d)] = "X" if (s == 0 or not same(s, d)) else "S"
    for s in partner:
        if s == 0:
            continue
        os_ = sum(CN[s][d] for d in R if cls.get((s, d)) == "S")
        ls_ = sum(CN[t][s] for t in R if cls.get((t, s)) == "S")
        if os_ + ls_ > W - HZ and cls.get((s, partner[s])) == "S":
            cls[(s, partner[s])] = "R"
    size = {k: [sum(CN[s][d] for s in R if cls.get((s, d)) == k) for d in R] for k in "XS"}
    land = {}
    runs = {"X": [[] for _ in R], "S": [[] for _ in R]}
    for d in R:
        col = {k: W - size[k][d] for k in "XS"}
        last = None
        for s in R:
            k = cls.get((s, d))
            if k is None:
                continue
            if k in "XS":
                land[(s, d)] = col[k]
                if last == k:
                    runs[k][d][-1][2] += CN[s][d]
                else:
                    runs[k][d].append([yo[d][s], col[k], CN[s][d]])
                col[k] += CN[s][d]
            last = k

    def pieces(w, lst, lsem):
        for c in sorted(set(CN[s][d] for _, s, d in lst), reverse=True):
            grp = [(d, land[(s, d)], sc, c) for sc, s, d in lst if CN[s][d] == c]
            while grp:
                snd(w, grp[:8], "a", lsem)
                grp = grp[8:]

    def xloads(r, c0, dsts, sem):
        pos = {}
        run = None
        c = c0
        for d in dsts:
            pos[d] = c
            if run and run[1] + run[2] == xo[r][d]:
                run[2] += CN[r][d]
            else:
                if run:
                    ld(r, run[0], run[1], run[2], sem)
                run = [c, xo[r][d], CN[r][d]]
            c += CN[r][d]
        if run:
            ld(r, run[0], run[1], run[2], sem)
        return pos

    G0 = [g for g in R if isG[g] and chip[g] == chip[0]]
    P0 = [p for p in R if p and not isG[p] and chip[p] == chip[0]][0]
    plane0 = [r for r in R if r and same(r, 0)]
    plane1 = [r for r in R if not same(r, 0)]
    far = [r for r in plane0 if chip[r] != chip[0]]
    hubs = {0: plane0}
    mate1 = [r for r in plane1 if topo.mates(chip[r], chip[0])]
    hop2 = [r for r in plane1 if r not in mate1]
    hub1 = [r for r in hop2 if not isG[r]][0]
    hubs[hub1] = [r for r in plane1 if r != hub1]
    hubof = {}
    for h in hubs:
        for r in hubs[h]:
            hubof[r] = h
    hs = lambda r: "c" if r == hub1 else "b"
    bs = lambda h: "b" if h == hub1 else "c"
    Ps = [p for p in R if p and not isG[p]]
    Gs = [g for g in R if isG[g]]
    Gn = [g for g in Gs if g not in G0]
    relay = lambda s, d: EXC.get((s, d), partner[s])
    part = {}
    for s in Ps:
        for d in R:
            if cls.get((s, d)) in ("X", "R"):
                part.setdefault((s, relay(s, d)), []).append(d)
    wid = lambda s, ds: sum(CN[s][d] for d in ds)
    own = {g: [d for d in R if cls.get((g, d)) == "X"] for g in Gs}
    end1 = [W - size["X"][r] for r in R]
    d0 = [d for d in R if small(0, d)]
    T0 = wid(0, d0)
    cut = min((max(xo[0][d], T0 - xo[0][d]), xo[0][d]) for d in d0)
    w0, cutx = cut
    grp0 = {G0[0]: [d for d in d0 if xo[0][d] < cutx], G0[1]: [d for d in d0 if xo[0][d] >= cutx]}
    x00 = {G0[0]: 0, G0[1]: T0 - w0}
    slot0 = {G0[0]: 0, P0: HZ, G0[1]: 2 * HZ}
    ri, wa0 = {}, {}
    for g in Gs:
        tot = sum(wid(s, part[(s, g)]) for s in Ps if (s, g) in part)
        need = max(w0, tot + wid(g, own[g])) if g in G0 else max(tot, wid(g, own[g]))
        wa0[g] = end1[g] - need
        c = wa0[g]
        for s in Ps:
            if (s, g) in part:
                ri[(s, g)] = c
                c += wid(s, part[(s, g)])
    sb, sb0 = {}, {}
    for s in Ps:
        tg = [g for g in Gs if (s, g) in part]
        sb0[s] = end1[s] - sum(wid(s, part[(s, g)]) for g in tg)

    def hot_ld(r, sem=None):
        if sem:
            wt(r, sem, "sync")
        ld(r, 0, 0, HZ, hs(r), "sync")

    def hot_to0(r, slot, high=False):
        snd(r, [(0, slot * HZ, 0, HZ)], "a", hs(r), high=high)

    def hot_mv(r, dst):
        snd(r, [(dst, 0, 0, HZ)], "b", hs(r))

    def fwd(g, srcs):
        lst = []
        for s in srcs:
            c = ri[(s, g)]
            for d in part[(s, g)]:
                if cls[(s, d)] == "X":
                    lst.append((c, s, d))
                c += CN[s][d]
        return lst

    def store0(blocks, early=None):
        wtq(0, "a")
        if early:
            wt(0, "a")
        i = 0
        while i < 3:
            j = i
            while j + 1 < 3 and blocks[j + 1] == blocks[j] + 1:
                j += 1
            st(0, yo[0][blocks[i]], i * HZ, (j - i + 1) * HZ, "a")
            i = j + 1
        if early:
            sg(0, early, "b", "a")

    m = {g: [p for p in Ps if partner[p] == g][0] for g in Gn}
    gm = [g for g in mate1 if isG[g]]
    gh = [g for g in hop2 if isG[g]]
    gf = [g for g in far if isG[g]]
    pf = [p for p in far if not isG[p]]

    for g in G0:
        ld(0, slot0[g], x00[g], w0, "b")
    early = G0 + [P0, gm[0], gf[0], m[gm[0]], m[gh[0]]]
    for r in early:
        hot_ld(r)
    for s in Ps:
        c = sb0[s]
        for g in Gs:
            if (s, g) in part:
                sb[(s, g)] = c
                xloads(s, c, part[(s, g)], "c")
                c += wid(s, part[(s, g)])
    late[0] = 1
    wt(0, "b")
    snd(0, [(g, wa0[g], slot0[g], w0) for g in G0], "b", "a")
    wt(P0, "b")
    hot_to0(P0, 1)
    for s in Ps:
        if s == P0:
            continue
        wt(s, "c")
        for g in Gs:
            if (s, g) in part:
                snd(s, [(g, ri[(s, g)], sb[(s, g)], wid(s, part[(s, g)]))], "c", "c")
    p4, p12, p6, p14 = m[gm[0]], m[gh[0]], m[gm[1]], m[gh[1]]
    wt(p4, "b")
    hot_mv(p4, gm[1])
    hot_mv(p12, gh[0])
    for g in G0:
        wt(g, "b")
        hot_to0(g, slot0[g] // HZ, high=True)
        pieces(g, [(wa0[g] + xo[0][d] - x00[g], 0, d) for d in grp0[g]], "c")
    for g in Gn:
        wt(g, "c")
        srcs = [s for s in Ps if (s, g) in part]
        pieces(g, fwd(g, srcs), "c")
        for s in srcs:
            c = ri[(s, g)]
            for d in part[(s, g)]:
                if cls[(s, d)] == "R":
                    wt(g, "c", "scalar")
                    st(g, yo[d][s], c, CN[s][d], "c", "scalar")
                c += CN[s][d]
    for s in Ps:
        if s not in early:
            hot_ld(s, "c")
    store0([G0[0], P0, G0[1]])
    up = {G0[0]: gm[0], G0[1]: gm[1]}
    ownpos = {}
    for g in G0:
        wt(g, "b")
        sg(g, [up[g], gf[0]], "b", "b")
        wt(g, "c")
        wtq(g, "c")
        sg(g, [P0], "c", "c")
        ownpos[g] = xloads(g, end1[g] - wid(g, own[g]), own[g], "c")
    for g in Gn:
        wtq(g, "c")
        ownpos[g] = xloads(g, end1[g] - wid(g, own[g]), own[g], "c")
    hot_ld(gf[1], "c")
    wt(p14, "b")
    hot_mv(p14, gh[1])
    wt(0, "a")
    ph2 = [pf[0], gf[0], pf[1]]
    sg(0, ph2, "b", "a")
    wt(P0, "c")
    for g in G0:
        if (P0, g) in part:
            snd(P0, [(g, ri[(P0, g)], sb[(P0, g)], wid(P0, part[(P0, g)]))], "c", "c")
    for g in gm:
        wt(g, "b")
        hot_mv(g, {gm[0]: G0[0], gm[1]: G0[1]}[g])
    for g in Gn:
        if g != gf[0]:
            wt(g, "c")
            pieces(g, [(ownpos[g][d], g, d) for d in own[g]], "c")
    for i, r in enumerate(ph2):
        wt(r, "b")
        hot_to0(r, i)
    wt(gf[0], "c")
    pieces(gf[0], [(ownpos[gf[0]][d], gf[0], d) for d in own[gf[0]]], "c")
    for g in G0:
        wt(g, "c")
        pieces(g, [(ownpos[g][d], g, d) for d in own[g]] + (fwd(g, [P0]) if (P0, g) in part else []), "c")
    wt(gm[0], "b")
    sg(gm[0], [p6, G0[0]], "b", "b")
    wt(p6, "b")
    hot_mv(p6, gm[0])
    hot_ld(gm[1], "b")
    wt(gm[1], "b")
    sg(gm[1], [G0[1]], "b", "b")
    for d in R:
        if d:
            wtq(d, "a")
            for y0, c0, w in runs["X"][d]:
                st(d, y0, c0, w, "a")
    store0(ph2, [gf[0]])
    wt(gf[0], "b")
    sg(gf[0], gh + [gf[1]], "b", "b")
    wt(0, "a")
    ph3 = [G0[1], G0[0], gf[1]]
    sg(0, ph3, "b", "a")
    wt(gh[0], "b")
    hot_mv(gh[0], pf[0])
    wt(gh[1], "b")
    hot_mv(gh[1], pf[1])
    for i, r in enumerate(ph3):
        wt(r, "b")
        hot_to0(r, i, high=True)
    for g in G0:
        wt(g, "b")
        sg(g, [up[g]], "b", "b")
    hot_ld(gh[0], "b")
    wt(gh[0], "b")
    hot_mv(gh[0], gf[0])
    hot_ld(gh[1], "b")
    wt(gh[1], "b")
    hot_mv(gh[1], P0)
    ospos = {}
    for r in R:
        if not r:
            continue
        wt(r, "c")
        wt(r, "a")
        wtq(r, "a")
        wtq(r, "c")
        if r in hubof:
            sg(r, [hubof[r]], bs(hubof[r]), "c")
        ospos[r] = xloads(r, HZ, [d for d in R if cls.get((r, d)) == "S"], "c")
    wt(hub1, "b")
    sg(hub1, hubs[hub1], "c", "c")
    store0([p4, gm[0], gf[1]])
    wt(0, "a")
    sg(0, ph2, "b", "a")
    wt(0, "c")
    sg(0, hubs[0], "c", "c")
    for i, r in enumerate(ph2):
        wt(r, "b")
        hot_to0(r, i)
    wt(gm[0], "b")
    hot_mv(gm[0], G0[0])
    wt(gm[1], "b")
    hot_mv(gm[1], G0[1])
    for r in R:
        if r:
            wt(r, "c")
            pieces(r, [(ospos[r][d], r, d) for d in ospos[r]], "c")
    store0([p12, gh[0], p14])
    wt(0, "a")
    ph5 = [G0[0], G0[1], P0]
    sg(0, ph5, "b", "a")
    for i, r in enumerate(ph5):
        wt(r, "b")
        hot_to0(r, i, high=True)
    for d in R:
        if d:
            wtq(d, "a")
            for y0, c0, w in runs["S"][d]:
                st(d, y0, c0, w, "a")
    store0([p6, gm[1], gh[1]])
    for r in R:
        for s in "abc":
            wt(r, s)
    return ops


def rank_program(g, core, T, topo):
    rank = T.rank_of(core)
    if rank is None:
        return
    from concourse.bass import DstId, RemoteDMATransfer
    B = T.buf
    Q = {"g": g, "sync": g.sync, "scalar": g.scalar}
    for op in build(T.tables, T.cores, topo):
        if op[0] != rank:
            continue
        k, q = op[1], Q[op[2]]
        if k == "ld":
            q.dma_start(B[:, op[3]:op[4]], T.x[:, op[5]:op[5] + op[4] - op[3]]).then_inc(T.sem[op[6]], 16)
        elif k == "st":
            q.dma_start(T.y[:, op[3]:op[3] + op[5] - op[4]], B[:, op[4]:op[5]]).then_inc(T.sem[op[6]], 16)
        elif k == "wt":
            q.wait_ge(T.sem[op[3]], op[4])
        elif k == "snd":
            trs, rs, ls = op[3], T.sem[op[4]], T.sem[op[5]]
            if len(trs) == 1:
                d, dc, sc, w, m = trs[0]
                rid, pid, _ = topo.addr(T.cores[d])
                g.remote_dma(B[:, dc:dc + w], B[:, sc:sc + w], rs, ls, pid, rid, m)
            else:
                lst = []
                for d, dc, sc, w, m in trs:
                    rid, pid, _ = topo.addr(T.cores[d])
                    lst.append(RemoteDMATransfer(dst_ids=[DstId(rid=rid, pnc=pid)], dma_engine_mask=m, remote_sem=rs,
                                                 src=B[:, sc:sc + w], dst=B[:, dc:dc + w]))
                g.remote_dma_fused(lst, local_sem=ls)
        elif k == "sg":
            ds, rs, ls = op[3], T.sem[op[4]], T.sem[op[5]]
            if len(ds) == 1:
                rid, pid, _ = topo.addr(T.cores[ds[0][0]])
                g.remote_sem_update(rs, ls, pid, rid, ds[0][1])
            else:
                lst = []
                for d, m in ds:
                    rid, pid, _ = topo.addr(T.cores[d])
                    lst.append(RemoteDMATransfer(dst_ids=[DstId(rid=rid, pnc=pid)], dma_engine_mask=m, remote_sem=rs))
                g.remote_dma_fused(lst, local_sem=ls)
